import numpy as np
import ml_dtypes


def mxq(x, axis, fmt="e4m3"):
    dtype, down = {"e4m3": (ml_dtypes.float8_e4m3fn, 7), "e5m2": (ml_dtypes.float8_e5m2, 14)}[fmt]
    v = np.moveaxis(np.asarray(x, np.float32).astype(ml_dtypes.bfloat16).astype(np.float64), axis, -1)
    blocks = v.reshape(v.shape[:-1] + (-1, 32))
    amax = np.abs(blocks).max(-1, keepdims=True)
    byte = np.maximum(np.where(amax > 0, np.frexp(amax)[1] - 1 + 127, 0) - down, 1)
    scale = np.exp2(byte - 127.0)
    codes = (blocks / scale).astype(np.float32).astype(dtype).astype(np.float64)
    return np.moveaxis((codes * scale).reshape(v.shape), -1, axis)


WIDE = False


def mx_kscale(k):
    if not WIDE:
        return np.ones(k)
    levels = np.array([10, -10, 5, -5, 0])
    if k % 512:
        return np.exp2(np.random.permutation(np.resize(levels, k // 32))).repeat(32)
    a = np.empty((k // 512, 16))
    for p in range(k // 512):
        a[p, :8] = np.random.permutation(np.resize(levels, 8))
        for g in range(8):
            far = levels[np.abs(levels - a[p, g]) >= 10]
            a[p, g + 8] = far[np.random.randint(len(far))]
    return np.exp2(a.ravel()).repeat(32)


def f64(x):
    return np.asarray(x).astype(np.float64)


def striped(idx):
    return np.tile(idx.reshape(-1, 16).T, (8, 1)).astype(np.uint16)


def unstriped(offs):
    return offs[:16].T.reshape(-1).astype(np.int64)


E2M1 = np.array([0.0, 0.5, 1.0, 1.5, 2.0, 3.0, 4.0, 6.0, -0.0, -0.5, -1.0, -1.5, -2.0, -3.0, -4.0, -6.0])


def pack_weight(w, fmt):
    k, n = w.shape
    w = f64(np.asarray(w, np.float32).astype(ml_dtypes.bfloat16)).reshape(k // 32, 32, n)
    amax = np.abs(w).max(1)
    if fmt == "e4m3":
        byte = np.frexp(amax)[1] - 1 + 127 - 7
    else:
        mant, ex = np.frexp(amax / 6.0)
        byte = np.where(mant > 0.5, ex, ex - 1) + 127
    byte = np.clip(np.where(amax > 0, byte, 1), 1, 254)
    scaled = (w * np.exp2(127.0 - byte)[:, None, :]).reshape(k, n).astype(np.float32)
    by_word = np.ascontiguousarray(scaled.reshape(k // 512, 128, 4, n).transpose(0, 1, 3, 2))
    if fmt == "e4m3":
        words = by_word.astype(ml_dtypes.float8_e4m3fn).view(np.uint8)
    else:
        c = by_word.astype(ml_dtypes.float4_e2m1fn).view(np.uint8) & 0xF
        words = (c[..., 0::2] | (c[..., 1::2] << 4)).reshape(k // 512, 128, 2 * n)
    return np.ascontiguousarray(words), np.ascontiguousarray(byte.astype(np.uint8).reshape(k // 512, 16, n))


def unpack_weight(words, scales, fmt):
    g, _, n = scales.shape
    words = np.ascontiguousarray(words).reshape(g, 128, n, -1)
    if fmt == "e4m3":
        vals = words.view(ml_dtypes.float8_e4m3fn).astype(np.float64)
    else:
        nib = np.empty((g, 128, n, 4), np.uint8)
        nib[..., 0::2] = words & 0xF
        nib[..., 1::2] = words >> 4
        vals = E2M1[nib]
    vals = vals * np.repeat(np.exp2(scales.astype(np.float64) - 127.0), 8, axis=1)[..., None]
    return vals.transpose(0, 1, 3, 2).reshape(g * 512, n)


def gelu(v):
    return 0.5 * v * (1.0 + np.tanh(np.sqrt(2.0 / np.pi) * (v + 0.044715 * v**3)))


def bf(x):
    return np.asarray(x, np.float32).astype(ml_dtypes.bfloat16)


def planes(Y):
    n, m = Y.shape
    b = f64(bf(Y)).reshape(n // 32, 32, m)
    amax = np.abs(b).max(1)
    byte = np.clip(np.where(amax > 0, np.frexp(amax)[1] - 1 + 127 - 7, 1), 1, 254)
    codes = (b * np.exp2(127.0 - byte)[:, None, :]).reshape(n, m).astype(np.float32).astype(ml_dtypes.float8_e4m3fn).view(np.uint8)
    words = codes.reshape(n // 512, 128, 4, m).transpose(0, 1, 3, 2)
    return np.ascontiguousarray(words), np.ascontiguousarray(byte.astype(np.uint8).reshape(n // 512, 16, m))


K, K2, H, N, T, S = 1024, 512, 1024, 512, 2048, 1024


def setup_inputs():
    n = np.random.standard_normal
    s = mx_kscale(K)[:, None]
    s2 = mx_kscale(K2)[:, None]
    u = mx_kscale(H)[:, None]
    d = {}
    d["tab_words"], d["tab_scales"] = pack_weight(n((K, T)) * s, "e4m3")
    d["offs"] = striped(np.random.permutation(T)[:S])
    d["xs_words"], d["xs_scales"] = pack_weight(n((K2, S)) * s2, "e4m3")
    d["w1"] = (1.2 * n((K, H)) / K**0.5 / s).astype(np.float32)
    d["w2"] = (0.55 * n((K2, H)) / K2**0.5 / s2).astype(np.float32)
    d["alt"] = (0.5 * n((H, S))).astype(np.float32)
    d["gain"] = (np.exp(0.3 * n(H)) * u[:, 0]).astype(np.float32)
    w3 = n((H, N)) / H**0.5 / u * np.exp(0.8 * n(N))
    d["w3_words"], d["w3_scales"] = pack_weight(w3, "e2m1")
    return d


def reference(tab_words, tab_scales, offs, xs_words, xs_scales, w1, w2, alt, gain, w3_words, w3_scales):
    v = unpack_weight(tab_words, tab_scales, "e4m3")[:, unstriped(offs)]
    xs = unpack_weight(xs_words, xs_scales, "e4m3")
    w3 = unpack_weight(w3_words, w3_scales, "e2m1")
    a = np.tanh(mxq(f64(w1), 0, "e4m3").T @ v)
    b = np.sin(mxq(f64(w2), 0, "e4m3").T @ xs)
    h = (a - b + f64(alt)) * f64(gain)[:, None]
    y = w3.T @ mxq(h, 0, "e4m3")
    words, scales = planes(y)
    return y, words, scales

@@ -1,0 +1,325 @@
+import math
+from contextlib import ExitStack
+
+import concourse.mybir as mybir
+from concourse.masks import make_identity
+
+K, K2, H, N, T, S = 1024, 512, 1024, 512, 2048, 1024
+FLOPS = 2 * S * (K * H + K2 * H + H * N)
+
+F32 = mybir.dt.float32
+BF16 = mybir.dt.bfloat16
+I32 = mybir.dt.int32
+U32 = mybir.dt.uint32
+U16 = mybir.dt.uint16
+U8 = mybir.dt.uint8
+FP8X4 = mybir.dt.float8_e4m3fn_x4
+FP4X4 = mybir.dt.float4_e2m1fn_x4
+ACT = mybir.ActivationFunctionType
+ALU = mybir.AluOpType
+
+P = 128
+PACK = 4
+PASS = P * PACK
+QUADS = 4
+SLICE = 256
+JT = S // P
+SCALAR_COLS = 96
+SCALAR_FROM = 6
+GROUPS = {0: (2, 2, 2, 2), 1: (2, 2, 2, 1, 1)}
+
+
+def tile_list_spirometry_breath_curve_kernel(
+    tc, tab_words, tab_scales, offs, xs_words, xs_scales, w1, w2, alt, gain, w3_words, w3_scales, out_0, out_1, out_2
+):
+    nc = tc.nc
+    with ExitStack() as ctx:
+        keep = ctx.enter_context(tc.tile_pool(name="keep", bufs=1))
+        work = ctx.enter_context(tc.tile_pool(name="work", bufs=2))
+        psum = ctx.enter_context(tc.psum_pool(name="psum", bufs=2))
+
+        def held(shape, dtype, name):
+            return keep.tile(shape, dtype, name=name, align_bytes=64)
+
+        offsets = keep.tile([P, S // 16], U16, name="offsets")
+        nc.sync.dma_start(offsets[:], offs)
+
+        xs_sc = held([P, S], U8, "xs_sc")
+        tab_sc = held([P, T], U8, "tab_sc")
+        w3_sc_raw = held([P, 2 * N], U8, "w3_sc_raw")
+        for plane in (xs_sc, tab_sc, w3_sc_raw):
+            nc.gpsimd.memset(plane[:].bitcast(I32), 0)
+
+        ident = held([P, P], F32, "ident")
+        make_identity(nc, ident[:])
+
+        zero_in = held([P, 1], F32, "zero_in")
+        zero = held([P, 1], F32, "zero")
+        phase = held([P, 1], F32, "phase")
+        root2 = held([P, 1], F32, "root2")
+        nc.vector.memset(zero_in[:], 0.0)
+        nc.scalar.activation(zero[:], zero_in[:], ACT.Silu)
+        nc.vector.tensor_scalar(phase[:], zero[:], math.pi / 8, None, ALU.add)
+        nc.vector.tensor_scalar(root2[:], zero[:], math.sqrt(2.0), None, ALU.add)
+
+        def load_weight(w, a, b, parts=1):
+            width = PASS // parts
+            pieces = []
+            for part in range(parts):
+                raw = work.tile([P, PACK, width], F32, name="w_raw%d" % parts, bufs=5 if parts == 1 else 2)
+                rows = w[a * PASS : (a + 1) * PASS, b * PASS + part * width : b * PASS + (part + 1) * width]
+                nc.sync.dma_start(raw[:], rows.rearrange("(p i) c -> p i c", i=PACK))
+                pieces.append(raw)
+            return pieces
+
+        alt_sb = {}
+
+        def load_alt(b, first, tiles):
+            rows = held([P, PACK, tiles * P], F32, "alt_%d_%d" % (b, first))
+            src = alt[b * PASS : (b + 1) * PASS, first * P : (first + tiles) * P]
+            nc.sync.dma_start(rows[:], src.rearrange("(p t) j -> p t j", t=PACK))
+            for jt in range(tiles):
+                alt_sb[(b, first + jt)] = rows[:, :, jt * P : (jt + 1) * P]
+
+        xs_w = held([P, S], U32, "xs_w")
+        xs_src = xs_words[0].rearrange("p c i -> p (c i)").bitcast(I32)
+        w_raw = {("w2", 0, 0): load_weight(w2, 0, 0, 2)}
+        nc.sync.dma_start(xs_w[:, :SLICE].bitcast(I32), xs_src[:, :SLICE])
+        for q in range(QUADS):
+            nc.sync.dma_start(xs_sc[32 * q : 32 * q + 4, :].bitcast(I32), xs_scales[0, 4 * q : 4 * q + 4, :].bitcast(I32))
+        nc.sync.dma_start(xs_w[:, SLICE:].bitcast(I32), xs_src[:, SLICE:])
+        tab_w = [held([P, T], U32, "tab_w%d" % a) for a in range(2)]
+
+        def load_table(a):
+            nc.sync.dma_start(tab_w[a][:].bitcast(I32), tab_words[a].rearrange("p c i -> p (c i)").bitcast(I32))
+
+        load_table(0)
+        for q in range(QUADS):
+            nc.sync.dma_start(tab_sc[32 * q : 32 * q + 8, :].bitcast(I32), tab_scales[:, 4 * q : 4 * q + 4, :].bitcast(I32))
+        w_raw[("w1", 0, 0)] = load_weight(w1, 0, 0)
+        w_raw[("w1", 1, 0)] = load_weight(w1, 1, 0)
+        load_table(1)
+        gains = held([P, 2, PACK], F32, "gains")
+        nc.sync.dma_start(gains[:], gain.rearrange("(b p t) -> p b t", b=2, t=PACK))
+        load_alt(0, 0, 2)
+        w_raw[("w2", 0, 1)] = load_weight(w2, 0, 1)
+        load_alt(0, 2, 2)
+        load_alt(0, 4, 4)
+        for a in range(2):
+            w_raw[("w1", a, 1)] = load_weight(w1, a, 1)
+        w3_raw = held([P, 2 * 2 * N], U8, "w3_raw")
+        nc.sync.dma_start(
+            w3_raw[:].bitcast(I32).rearrange("p (a n) -> p a n", a=2), w3_words.rearrange("a p n -> p a n").bitcast(I32)
+        )
+        for q in range(QUADS):
+            nc.sync.dma_start(
+                w3_sc_raw[32 * q : 32 * q + 4, :].bitcast(I32).rearrange("r (a n) -> r a n", a=2),
+                w3_scales[:, 4 * q : 4 * q + 4, :].rearrange("a r n -> r a n").bitcast(I32),
+            )
+        load_alt(1, 0, 4)
+        load_alt(1, 4, 4)
+
+        w_codes, w_sc = {}, {}
+
+        def quantize_weight(key, scalar_halves=()):
+            w_codes[key] = held([P, PASS], U32, "codes_%s_%d_%d" % key)
+            w_sc[key] = held([P, PASS], U8, "scales_%s_%d_%d" % key)
+            width = PASS // len(w_raw[key])
+            for part, raw in enumerate(w_raw[key]):
+                grouped = work.tile([P, width, PACK], BF16, name="w_grouped", bufs=3, align_bytes=64)
+                cut = width - SCALAR_COLS if part in scalar_halves else width
+                nc.vector.tensor_copy(
+                    grouped[:, :cut, :].rearrange("p (c n) i -> p c i n", n=4),
+                    raw[:, :, :cut].rearrange("p i (c n) -> p c i n", n=4),
+                )
+                if cut < width:
+                    nc.scalar.copy(
+                        grouped[:, cut:, :].rearrange("p (c n) i -> p c i n", n=4),
+                        raw[:, :, cut:].rearrange("p i (c n) -> p c i n", n=4),
+                    )
+                cols = slice(part * width, (part + 1) * width)
+                nc.vector.quantize_mx(
+                    out=w_codes[key][:, cols].bitcast(FP8X4),
+                    scales=w_sc[key][:, cols],
+                    in_=grouped[:].rearrange("p c i -> p (c i)"),
+                )
+
+        picked_w, picked_sc = {}, {}
+
+        def gather(jq):
+            part = offsets[:, jq * SLICE // 16 : (jq + 1) * SLICE // 16]
+            for a in range(2):
+                picked_w[(a, jq)] = held([P, SLICE], U32, "picked_w%d_%d" % (a, jq))
+                nc.vector.tensor_copy(picked_w[(a, jq)][:], tab_w[a][:].indirect(part))
+            picked_sc[jq] = held([P, SLICE], U8, "picked_sc%d" % jq)
+            nc.vector.tensor_copy(picked_sc[jq][:], tab_sc[:].indirect(part))
+
+        tanh_t, wave_t = {}, {}
+
+        def tanh_branch(step):
+            b, jt = divmod(step, JT)
+            jq, cols = jt // 2, slice((jt % 2) * P, (jt % 2 + 1) * P)
+            acc = psum.tile([P, PASS], F32, name="acc_tanh")
+            for a in (1, 0):
+                nc.tensor.matmul_mx(
+                    out=acc[:],
+                    lhsT=picked_w[(a, jq)][:, cols].bitcast(FP8X4),
+                    lhsT_scale=picked_sc[jq][4 * a : P, cols],
+                    rhs=w_codes[("w1", a, b)][:].bitcast(FP8X4),
+                    rhs_scale=w_sc[("w1", a, b)][:],
+                    start=(a == 1),
+                    stop=(a == 0),
+                )
+            tanh_t[step] = work.tile([P, PACK, P], F32, name="tanh_t", bufs=4)
+            nc.scalar.activation(tanh_t[step][:], acc[:].rearrange("j (p t) -> j t p", t=PACK), ACT.Tanh)
+
+        def sine_branch(step):
+            b, jt = divmod(step, JT)
+            cols = slice(jt * P, (jt + 1) * P)
+            acc = psum.tile([P, PASS], F32, name="acc_sine", tag="sine_then_y", bufs=4)
+            nc.tensor.matmul_mx(
+                out=acc[:],
+                lhsT=xs_w[:, cols].bitcast(FP8X4),
+                lhsT_scale=xs_sc[:, cols],
+                rhs=w_codes[("w2", 0, b)][:].bitcast(FP8X4),
+                rhs_scale=w_sc[("w2", 0, b)][:],
+                start=True,
+                stop=True,
+            )
+            quarter = work.tile([P, PACK, P], F32, name="quarter", bufs=2)
+            nc.scalar.activation(
+                quarter[:], acc[:].rearrange("j (p t) -> j t p", t=PACK), ACT.Sin, bias=phase[:], scale=0.25
+            )
+            squared = work.tile([P, PACK, P], F32, name="squared", bufs=2)
+            nc.scalar.activation(squared[:], quarter[:], ACT.Square)
+            wave_t[step] = work.tile([P, PACK, P], F32, name="wave_t", bufs=9)
+            nc.scalar.activation(wave_t[step][:], squared[:], ACT.Square, bias=root2[:], scale=-2.0 * math.sqrt(2.0))
+
+        h_codes = [held([P, S], U32, "h_codes%d" % b) for b in range(2)]
+        h_sc = [held([P, S], U8, "h_sc%d" % b) for b in range(2)]
+        y_codes = held([P, S], U32, "y_codes")
+        y_sc = held([P, S], U8, "y_sc")
+        w3_w = [held([P, 2 * N], U8, "w3_w%d" % b) for b in range(2)]
+        w3_sc = [held([P, N], U8, "w3_sc%d" % b) for b in range(2)]
+
+        def deal_w3(b):
+            nc.vector.tensor_copy(
+                w3_w[b][:].rearrange("p (t o q e) -> p o t q e", t=PACK, q=8, e=2),
+                w3_raw[:, b * 2 * N : (b + 1) * 2 * N].rearrange("p (o q t e) -> p o t q e", t=PACK, q=8, e=2),
+            )
+            nc.vector.tensor_copy(
+                w3_sc[b][:].rearrange("p (t o q) -> p o t q", t=PACK, q=16),
+                w3_sc_raw[:, b * N : (b + 1) * N].rearrange("p (o q t) -> p o t q", t=PACK, q=16),
+            )
+
+        def join(step, total, place):
+            b, jt = divmod(step, JT)
+            both = psum.tile([P, PACK, P], F32, name="both")
+            for t in range(PACK):
+                nc.tensor.matmul(both[:, t, :], wave_t[step][:, t, :], ident[:], start=True, stop=False, is_transpose=True)
+                nc.tensor.matmul(both[:, t, :], tanh_t[step][:, t, :], ident[:], start=False, stop=True, is_transpose=True)
+            nc.vector.scalar_tensor_tensor(
+                total[:, :, place * P : (place + 1) * P],
+                both[:],
+                -1.0,
+                alt_sb[(b, jt)],
+                ALU.add,
+                ALU.add,
+            )
+
+        def quantize_h(b, total, cols):
+            width = cols.stop - cols.start
+            grouped = work.tile([P, width, PACK], BF16, name="h_grouped", bufs=3, align_bytes=64)
+            nc.vector.tensor_tensor(
+                grouped[:].rearrange("p (c n) t -> p c t n", n=4),
+                total[:].rearrange("p t (c n) -> p c t n", n=4),
+                gains[:, b, :].unsqueeze(1).unsqueeze(3).to_broadcast([P, width // 4, PACK, 4]),
+                ALU.mult,
+            )
+            nc.vector.quantize_mx(
+                out=h_codes[b][:, cols].bitcast(FP8X4), scales=h_sc[b][:, cols], in_=grouped[:].rearrange("p c t -> p (c t)")
+            )
+
+        out_rows = out_0.rearrange("(p t) j -> p t j", t=PACK)
+        out_words = out_1[0].rearrange("p m t -> p (m t)").bitcast(I32)
+
+        def features(cols, late):
+            width = cols.stop - cols.start
+            part = P if late else width
+            per_bank = PASS // part
+            y = work.tile([P, PACK, width], F32, name="y", bufs=2)
+            grouped = work.tile([P, width, PACK], BF16, name="y_grouped", bufs=2, align_bytes=64)
+            for j0 in range(0, width, part):
+                moving = slice(cols.start + j0, cols.start + j0 + part)
+                for t0 in range(0, PACK, per_bank):
+                    acc = psum.tile([P, per_bank, part], F32, name="acc_y", tag="sine_then_y", bufs=4)
+                    for t in range(t0, t0 + per_bank):
+                        for b in range(2):
+                            nc.tensor.matmul_mx(
+                                out=acc[:, t - t0, :],
+                                lhsT=w3_w[b][:, t * 2 * P : (t + 1) * 2 * P].bitcast(FP4X4),
+                                lhsT_scale=w3_sc[b][:, t * P : (t + 1) * P],
+                                rhs=h_codes[b][:, moving].bitcast(FP8X4),
+                                rhs_scale=h_sc[b][:, moving],
+                                start=(b == 0),
+                                stop=(b == 1),
+                            )
+                    if late:
+                        nc.scalar.copy(grouped[:, j0 : j0 + P, :], acc[:].rearrange("p t j -> p j t"))
+                        nc.scalar.copy(y[:, :, j0 : j0 + P], acc[:])
+                    else:
+                        nc.scalar.copy(y[:, t0 : t0 + per_bank, :], acc[:])
+            if not late:
+                nc.vector.tensor_copy(
+                    grouped[:].rearrange("p (c n) t -> p c t n", n=4), y[:].rearrange("p t (c n) -> p c t n", n=4)
+                )
+            nc.vector.quantize_mx(
+                out=y_codes[:, cols].bitcast(FP8X4), scales=y_sc[:, cols], in_=grouped[:].rearrange("p c t -> p (c t)")
+            )
+            nc.sync.dma_start(out_rows[:, :, cols], y[:])
+            nc.sync.dma_start(out_words[:, cols], y_codes[:, cols].bitcast(I32))
+
+        TANH_AHEAD, SINE_AHEAD, SINE_FIRST = 2, 4, 7
+        quantize_weight(("w2", 0, 0), (0, 1))
+        for step in range(SINE_FIRST):
+            sine_branch(step)
+        quantize_weight(("w1", 0, 0))
+        quantize_weight(("w1", 1, 0))
+        gather(0)
+        for step in range(TANH_AHEAD):
+            tanh_branch(step)
+        extras = {
+            0: lambda: gather(1),
+            1: lambda: quantize_weight(("w2", 0, 1)),
+            2: lambda: gather(2),
+            3: lambda: quantize_weight(("w1", 0, 1)),
+            4: lambda: gather(3),
+            5: lambda: quantize_weight(("w1", 1, 1)),
+            6: lambda: deal_w3(0),
+            7: lambda: deal_w3(1),
+        }
+        step = 0
+        ready = []
+        for b in range(2):
+            jt = 0
+            for tiles in GROUPS[b]:
+                total = work.tile([P, PACK, tiles * P], F32, name="total", bufs=3)
+                for place in range(tiles):
+                    if step in extras:
+                        extras[step]()
+                    if step + TANH_AHEAD < 2 * JT:
+                        tanh_branch(step + TANH_AHEAD)
+                    join(step, total, place)
+                    if ready:
+                        features(*ready.pop())
+                    if SINE_FIRST <= step + SINE_AHEAD < 2 * JT:
+                        sine_branch(step + SINE_AHEAD)
+                    step += 1
+                cols = slice(jt * P, (jt + tiles) * P)
+                quantize_h(b, total, cols)
+                if b == 1:
+                    ready.append((cols, jt >= SCALAR_FROM))
+                jt += tiles
+        features(*ready.pop())
+        for q in range(QUADS):
+            nc.sync.dma_start(out_2[0, 4 * q : 4 * q + 4, :].bitcast(I32), y_sc[32 * q : 32 * q + 4, :].bitcast(I32))

@@ -26,7 +26,8 @@ SLICE = 256
 JT = S // P
 SCALAR_COLS = 96
 SCALAR_FROM = 6
-GROUPS = {0: (2, 2, 2, 2), 1: (2, 2, 2, 1, 1)}
+CODE_STORES = {512: 0, 1024: 512}
+GROUPS = ((0, 0, 1), (0, 1, 1), (0, 2, 2), (0, 4, 2), (0, 6, 2), (1, 0, 2), (1, 2, 2), (1, 4, 2), (1, 6, 1), (1, 7, 1))
 
 
 def tile_list_spirometry_breath_curve_kernel(
@@ -66,7 +67,7 @@ def tile_list_spirometry_breath_curve_kernel(
             width = PASS // parts
             pieces = []
             for part in range(parts):
-                raw = work.tile([P, PACK, width], F32, name="w_raw%d" % parts, bufs=5 if parts == 1 else 2)
+                raw = work.tile([P, PACK, width], F32, name="w_raw%d" % parts, bufs=4 if parts == 1 else 2)
                 rows = w[a * PASS : (a + 1) * PASS, b * PASS + part * width : b * PASS + (part + 1) * width]
                 nc.sync.dma_start(raw[:], rows.rearrange("(p i) c -> p i c", i=PACK))
                 pieces.append(raw)
@@ -83,31 +84,36 @@ def tile_list_spirometry_breath_curve_kernel(
 
         xs_w = held([P, S], U32, "xs_w")
         xs_src = xs_words[0].rearrange("p c i -> p (c i)").bitcast(I32)
-        w_raw = {("w2", 0, 0): load_weight(w2, 0, 0, 2)}
-        nc.sync.dma_start(xs_w[:, :SLICE].bitcast(I32), xs_src[:, :SLICE])
-        for q in range(QUADS):
-            nc.sync.dma_start(xs_sc[32 * q : 32 * q + 4, :].bitcast(I32), xs_scales[0, 4 * q : 4 * q + 4, :].bitcast(I32))
-        nc.sync.dma_start(xs_w[:, SLICE:].bitcast(I32), xs_src[:, SLICE:])
         tab_w = [held([P, T], U32, "tab_w%d" % a) for a in range(2)]
+        gains = held([P, 2, PACK], F32, "gains")
+        w3_raw = held([P, 2 * 2 * N], U8, "w3_raw")
+        w_raw = {}
+
+        def load_xs(first, tiles):
+            cols = slice(first * P, (first + tiles) * P)
+            nc.sync.dma_start(xs_w[:, cols].bitcast(I32), xs_src[:, cols])
 
         def load_table(a):
             nc.sync.dma_start(tab_w[a][:].bitcast(I32), tab_words[a].rearrange("p c i -> p (c i)").bitcast(I32))
 
+        w_raw[("w2", 0, 0)] = load_weight(w2, 0, 0, 2)
+        load_xs(0, 2)
+        for q in range(QUADS):
+            nc.sync.dma_start(xs_sc[32 * q : 32 * q + 4, :].bitcast(I32), xs_scales[0, 4 * q : 4 * q + 4, :].bitcast(I32))
+        load_xs(2, 6)
         load_table(0)
         for q in range(QUADS):
             nc.sync.dma_start(tab_sc[32 * q : 32 * q + 8, :].bitcast(I32), tab_scales[:, 4 * q : 4 * q + 4, :].bitcast(I32))
         w_raw[("w1", 0, 0)] = load_weight(w1, 0, 0)
         w_raw[("w1", 1, 0)] = load_weight(w1, 1, 0)
         load_table(1)
-        gains = held([P, 2, PACK], F32, "gains")
         nc.sync.dma_start(gains[:], gain.rearrange("(b p t) -> p b t", b=2, t=PACK))
         load_alt(0, 0, 2)
         w_raw[("w2", 0, 1)] = load_weight(w2, 0, 1)
         load_alt(0, 2, 2)
         load_alt(0, 4, 4)
-        for a in range(2):
-            w_raw[("w1", a, 1)] = load_weight(w1, a, 1)
-        w3_raw = held([P, 2 * 2 * N], U8, "w3_raw")
+        w_raw[("w1", 0, 1)] = load_weight(w1, 0, 1)
+        w_raw[("w1", 1, 1)] = load_weight(w1, 1, 1)
         nc.sync.dma_start(
             w3_raw[:].bitcast(I32).rearrange("p (a n) -> p a n", a=2), w3_words.rearrange("a p n -> p a n").bitcast(I32)
         )
@@ -121,17 +127,18 @@ def tile_list_spirometry_breath_curve_kernel(
 
         w_codes, w_sc = {}, {}
 
-        def quantize_weight(key, scalar_halves=()):
+        def quantize_weight(key, scalar_cols=0):
             w_codes[key] = held([P, PASS], U32, "codes_%s_%d_%d" % key)
             w_sc[key] = held([P, PASS], U8, "scales_%s_%d_%d" % key)
             width = PASS // len(w_raw[key])
             for part, raw in enumerate(w_raw[key]):
                 grouped = work.tile([P, width, PACK], BF16, name="w_grouped", bufs=3, align_bytes=64)
-                cut = width - SCALAR_COLS if part in scalar_halves else width
-                nc.vector.tensor_copy(
-                    grouped[:, :cut, :].rearrange("p (c n) i -> p c i n", n=4),
-                    raw[:, :, :cut].rearrange("p i (c n) -> p c i n", n=4),
-                )
+                cut = width - scalar_cols
+                if cut > 0:
+                    nc.vector.tensor_copy(
+                        grouped[:, :cut, :].rearrange("p (c n) i -> p c i n", n=4),
+                        raw[:, :, :cut].rearrange("p i (c n) -> p c i n", n=4),
+                    )
                 if cut < width:
                     nc.scalar.copy(
                         grouped[:, cut:, :].rearrange("p (c n) i -> p c i n", n=4),
@@ -157,9 +164,9 @@ def tile_list_spirometry_breath_curve_kernel(
         tanh_t, wave_t = {}, {}
 
         def tanh_branch(step):
-            b, jt = divmod(step, JT)
+            b, jt = step
             jq, cols = jt // 2, slice((jt % 2) * P, (jt % 2 + 1) * P)
-            acc = psum.tile([P, PASS], F32, name="acc_tanh")
+            acc = psum.tile([P, PASS], F32, name="acc_tanh", bufs=2)
             for a in (1, 0):
                 nc.tensor.matmul_mx(
                     out=acc[:],
@@ -174,9 +181,9 @@ def tile_list_spirometry_breath_curve_kernel(
             nc.scalar.activation(tanh_t[step][:], acc[:].rearrange("j (p t) -> j t p", t=PACK), ACT.Tanh)
 
         def sine_branch(step):
-            b, jt = divmod(step, JT)
+            b, jt = step
             cols = slice(jt * P, (jt + 1) * P)
-            acc = psum.tile([P, PASS], F32, name="acc_sine", tag="sine_then_y", bufs=4)
+            acc = psum.tile([P, PASS], F32, name="acc_sine", tag="sine_then_y", bufs=3)
             nc.tensor.matmul_mx(
                 out=acc[:],
                 lhsT=xs_w[:, cols].bitcast(FP8X4),
@@ -203,9 +210,9 @@ def tile_list_spirometry_breath_curve_kernel(
         w3_sc = [held([P, N], U8, "w3_sc%d" % b) for b in range(2)]
 
         def deal_w3(b):
-            nc.vector.tensor_copy(
-                w3_w[b][:].rearrange("p (t o q e) -> p o t q e", t=PACK, q=8, e=2),
-                w3_raw[:, b * 2 * N : (b + 1) * 2 * N].rearrange("p (o q t e) -> p o t q e", t=PACK, q=8, e=2),
+            nc.scalar.copy(
+                w3_w[b][:].bitcast(U16).rearrange("p (t o q) -> p o t q", t=PACK, q=8),
+                w3_raw[:, b * 2 * N : (b + 1) * 2 * N].bitcast(U16).rearrange("p (o q t) -> p o t q", t=PACK, q=8),
             )
             nc.vector.tensor_copy(
                 w3_sc[b][:].rearrange("p (t o q) -> p o t q", t=PACK, q=16),
@@ -213,8 +220,8 @@ def tile_list_spirometry_breath_curve_kernel(
             )
 
         def join(step, total, place):
-            b, jt = divmod(step, JT)
-            both = psum.tile([P, PACK, P], F32, name="both")
+            b, jt = step
+            both = psum.tile([P, PACK, P], F32, name="both", bufs=3)
             for t in range(PACK):
                 nc.tensor.matmul(both[:, t, :], wave_t[step][:, t, :], ident[:], start=True, stop=False, is_transpose=True)
                 nc.tensor.matmul(both[:, t, :], tanh_t[step][:, t, :], ident[:], start=False, stop=True, is_transpose=True)
@@ -247,12 +254,12 @@ def tile_list_spirometry_breath_curve_kernel(
             width = cols.stop - cols.start
             part = P if late else width
             per_bank = PASS // part
-            y = work.tile([P, PACK, width], F32, name="y", bufs=2)
-            grouped = work.tile([P, width, PACK], BF16, name="y_grouped", bufs=2, align_bytes=64)
+            y = work.tile([P, PACK, width], F32, name="y", bufs=5)
+            grouped = work.tile([P, width, PACK], BF16, name="y_grouped", bufs=3, align_bytes=64)
             for j0 in range(0, width, part):
                 moving = slice(cols.start + j0, cols.start + j0 + part)
                 for t0 in range(0, PACK, per_bank):
-                    acc = psum.tile([P, per_bank, part], F32, name="acc_y", tag="sine_then_y", bufs=4)
+                    acc = psum.tile([P, per_bank, part], F32, name="acc_y", tag="sine_then_y", bufs=3)
                     for t in range(t0, t0 + per_bank):
                         for b in range(2):
                             nc.tensor.matmul_mx(
@@ -277,49 +284,51 @@ def tile_list_spirometry_breath_curve_kernel(
                 out=y_codes[:, cols].bitcast(FP8X4), scales=y_sc[:, cols], in_=grouped[:].rearrange("p c t -> p (c t)")
             )
             nc.sync.dma_start(out_rows[:, :, cols], y[:])
-            nc.sync.dma_start(out_words[:, cols], y_codes[:, cols].bitcast(I32))
+            if cols.stop in CODE_STORES:
+                done = slice(CODE_STORES[cols.stop], cols.stop)
+                nc.sync.dma_start(out_words[:, done], y_codes[:, done].bitcast(I32))
 
-        TANH_AHEAD, SINE_AHEAD, SINE_FIRST = 2, 4, 7
-        quantize_weight(("w2", 0, 0), (0, 1))
-        for step in range(SINE_FIRST):
+        TANH_AHEAD, SINE_AHEAD, SINE_FIRST, Y_LAG = 2, 4, 7, 5
+        steps = [(b, jt) for b, first, tiles in GROUPS for jt in range(first, first + tiles)]
+        sines = steps
+        quantize_weight(("w2", 0, 0), 96)
+        for step in sines[:SINE_FIRST]:
             sine_branch(step)
-        quantize_weight(("w1", 0, 0))
-        quantize_weight(("w1", 1, 0))
+        quantize_weight(("w1", 0, 0), 0)
+        quantize_weight(("w1", 1, 0), 0)
         gather(0)
-        for step in range(TANH_AHEAD):
+        for step in steps[:TANH_AHEAD]:
             tanh_branch(step)
         extras = {
-            0: lambda: gather(1),
-            1: lambda: quantize_weight(("w2", 0, 1)),
-            2: lambda: gather(2),
-            3: lambda: quantize_weight(("w1", 0, 1)),
-            4: lambda: gather(3),
-            5: lambda: quantize_weight(("w1", 1, 1)),
-            6: lambda: deal_w3(0),
-            7: lambda: deal_w3(1),
+            0: lambda: (gather(1),),
+            1: lambda: (quantize_weight(("w2", 0, 1), 0),),
+            2: lambda: (gather(2),),
+            3: lambda: (quantize_weight(("w1", 0, 1), 0),),
+            4: lambda: (gather(3),),
+            5: lambda: (quantize_weight(("w1", 1, 1), 0),),
+            6: lambda: (deal_w3(0),),
+            7: lambda: (deal_w3(1),),
         }
-        step = 0
+        count = 0
         ready = []
-        for b in range(2):
-            jt = 0
-            for tiles in GROUPS[b]:
-                total = work.tile([P, PACK, tiles * P], F32, name="total", bufs=3)
-                for place in range(tiles):
-                    if step in extras:
-                        extras[step]()
-                    if step + TANH_AHEAD < 2 * JT:
-                        tanh_branch(step + TANH_AHEAD)
-                    join(step, total, place)
-                    if ready:
-                        features(*ready.pop())
-                    if SINE_FIRST <= step + SINE_AHEAD < 2 * JT:
-                        sine_branch(step + SINE_AHEAD)
-                    step += 1
-                cols = slice(jt * P, (jt + tiles) * P)
-                quantize_h(b, total, cols)
-                if b == 1:
-                    ready.append((cols, jt >= SCALAR_FROM))
-                jt += tiles
-        features(*ready.pop())
+        for b, first, tiles in GROUPS:
+            total = work.tile([P, PACK, tiles * P], F32, name="total", bufs=3)
+            for place in range(tiles):
+                if count in extras:
+                    extras[count]()
+                if count + TANH_AHEAD < len(steps):
+                    tanh_branch(steps[count + TANH_AHEAD])
+                join(steps[count], total, place)
+                if SINE_FIRST <= count + SINE_AHEAD < len(steps):
+                    sine_branch(sines[count + SINE_AHEAD])
+                count += 1
+            cols = slice(first * P, (first + tiles) * P)
+            quantize_h(b, total, cols)
+            if b == 1:
+                ready.append((cols, first >= SCALAR_FROM))
+                if len(ready) > Y_LAG:
+                    features(*ready.pop(0))
+        for cols, late in ready:
+            features(cols, late)
         for q in range(QUADS):
             nc.sync.dma_start(out_2[0, 4 * q : 4 * q + 4, :].bitcast(I32), y_sc[32 * q : 32 * q + 4, :].bitcast(I32))

@@ -23,11 +23,12 @@ PACK = 4
 PASS = P * PACK
 QUADS = 4
 SLICE = 256
-JT = S // P
+LIST_ROWS = 16
+TANH_AHEAD = 2
+SINE_AHEAD = 4
+SINE_FIRST = 6
 SCALAR_COLS = 96
-SCALAR_FROM = 6
-CODE_STORES = {512: 0, 1024: 512}
-GROUPS = ((0, 0, 1), (0, 1, 1), (0, 2, 2), (0, 4, 2), (0, 6, 2), (1, 0, 2), (1, 2, 2), (1, 4, 2), (1, 6, 1), (1, 7, 1))
+CODE_STORE = 512
 
 
 def tile_list_spirometry_breath_curve_kernel(
@@ -42,7 +43,7 @@ def tile_list_spirometry_breath_curve_kernel(
         def held(shape, dtype, name):
             return keep.tile(shape, dtype, name=name, align_bytes=64)
 
-        offsets = keep.tile([P, S // 16], U16, name="offsets")
+        offsets = keep.tile([P, S // LIST_ROWS], U16, name="offsets")
         nc.sync.dma_start(offsets[:], offs)
 
         xs_sc = held([P, S], U8, "xs_sc")
@@ -63,17 +64,20 @@ def tile_list_spirometry_breath_curve_kernel(
         nc.vector.tensor_scalar(phase[:], zero[:], math.pi / 8, None, ALU.add)
         nc.vector.tensor_scalar(root2[:], zero[:], math.sqrt(2.0), None, ALU.add)
 
-        def load_weight(w, a, b, parts=1):
-            width = PASS // parts
-            pieces = []
-            for part in range(parts):
-                raw = work.tile([P, PACK, width], F32, name="w_raw%d" % parts, bufs=4 if parts == 1 else 2)
-                rows = w[a * PASS : (a + 1) * PASS, b * PASS + part * width : b * PASS + (part + 1) * width]
-                nc.sync.dma_start(raw[:], rows.rearrange("(p i) c -> p i c", i=PACK))
-                pieces.append(raw)
-            return pieces
+        xs_w = held([P, S], U32, "xs_w")
+        tab_w = [held([P, T], U32, "tab_w%d" % a) for a in range(2)]
+        w3_raw = held([P, 2 * 2 * N], U8, "w3_raw")
+        gains = held([P, 2, PACK], F32, "gains")
+        w_raw, alt_sb = {}, {}
 
-        alt_sb = {}
+        def load_weight(name, w, a, b, pieces):
+            width = PASS // pieces
+            w_raw[(name, a, b)] = []
+            for piece in range(pieces):
+                raw = work.tile([P, PACK, width], F32, name="w_raw%d" % pieces, bufs=5 if pieces == 1 else 2)
+                rows = w[a * PASS : (a + 1) * PASS, b * PASS + piece * width : b * PASS + (piece + 1) * width]
+                nc.sync.dma_start(raw[:], rows.rearrange("(p i) c -> p i c", i=PACK))
+                w_raw[(name, a, b)].append(raw)
 
         def load_alt(b, first, tiles):
             rows = held([P, PACK, tiles * P], F32, "alt_%d_%d" % (b, first))
@@ -82,79 +86,70 @@ def tile_list_spirometry_breath_curve_kernel(
             for jt in range(tiles):
                 alt_sb[(b, first + jt)] = rows[:, :, jt * P : (jt + 1) * P]
 
-        xs_w = held([P, S], U32, "xs_w")
-        xs_src = xs_words[0].rearrange("p c i -> p (c i)").bitcast(I32)
-        tab_w = [held([P, T], U32, "tab_w%d" % a) for a in range(2)]
-        gains = held([P, 2, PACK], F32, "gains")
-        w3_raw = held([P, 2 * 2 * N], U8, "w3_raw")
-        w_raw = {}
-
-        def load_xs(first, tiles):
-            cols = slice(first * P, (first + tiles) * P)
-            nc.sync.dma_start(xs_w[:, cols].bitcast(I32), xs_src[:, cols])
+        def load_xs(cols):
+            src = xs_words[0].rearrange("p c i -> p (c i)").bitcast(I32)
+            nc.sync.dma_start(xs_w[:, cols].bitcast(I32), src[:, cols])
 
         def load_table(a):
             nc.sync.dma_start(tab_w[a][:].bitcast(I32), tab_words[a].rearrange("p c i -> p (c i)").bitcast(I32))
 
-        w_raw[("w2", 0, 0)] = load_weight(w2, 0, 0, 2)
-        load_xs(0, 2)
+        load_weight("w2", w2, 0, 0, 2)
+        load_xs(slice(0, SLICE))
         for q in range(QUADS):
             nc.sync.dma_start(xs_sc[32 * q : 32 * q + 4, :].bitcast(I32), xs_scales[0, 4 * q : 4 * q + 4, :].bitcast(I32))
-        load_xs(2, 6)
-        load_table(0)
-        for q in range(QUADS):
-            nc.sync.dma_start(tab_sc[32 * q : 32 * q + 8, :].bitcast(I32), tab_scales[:, 4 * q : 4 * q + 4, :].bitcast(I32))
-        w_raw[("w1", 0, 0)] = load_weight(w1, 0, 0)
-        w_raw[("w1", 1, 0)] = load_weight(w1, 1, 0)
-        load_table(1)
-        nc.sync.dma_start(gains[:], gain.rearrange("(b p t) -> p b t", b=2, t=PACK))
-        load_alt(0, 0, 2)
-        w_raw[("w2", 0, 1)] = load_weight(w2, 0, 1)
-        load_alt(0, 2, 2)
-        load_alt(0, 4, 4)
-        w_raw[("w1", 0, 1)] = load_weight(w1, 0, 1)
-        w_raw[("w1", 1, 1)] = load_weight(w1, 1, 1)
         nc.sync.dma_start(
             w3_raw[:].bitcast(I32).rearrange("p (a n) -> p a n", a=2), w3_words.rearrange("a p n -> p a n").bitcast(I32)
         )
+        load_xs(slice(SLICE, S))
+        load_table(0)
+        for q in range(QUADS):
+            nc.sync.dma_start(tab_sc[32 * q : 32 * q + 8, :].bitcast(I32), tab_scales[:, 4 * q : 4 * q + 4, :].bitcast(I32))
+        load_weight("w1", w1, 0, 0, 1)
+        load_weight("w1", w1, 1, 0, 1)
+        load_table(1)
+        load_weight("w2", w2, 0, 1, 1)
+        load_alt(0, 0, 2)
+        nc.sync.dma_start(gains[:], gain.rearrange("(b p t) -> p b t", b=2, t=PACK))
         for q in range(QUADS):
             nc.sync.dma_start(
                 w3_sc_raw[32 * q : 32 * q + 4, :].bitcast(I32).rearrange("r (a n) -> r a n", a=2),
                 w3_scales[:, 4 * q : 4 * q + 4, :].rearrange("a r n -> r a n").bitcast(I32),
             )
+        load_alt(0, 2, 2)
+        load_weight("w1", w1, 0, 1, 1)
+        load_alt(0, 4, 4)
+        load_weight("w1", w1, 1, 1, 1)
         load_alt(1, 0, 4)
         load_alt(1, 4, 4)
 
+        def innermost(rows, run):
+            return rows.rearrange("p (c n) t -> p c t n", n=run)
+
+        def outermost(rows, run):
+            return rows.rearrange("p t (c n) -> p c t n", n=run)
+
+        def quantize(codes, scales, grouped):
+            nc.vector.quantize_mx(out=codes.bitcast(FP8X4), scales=scales, in_=grouped[:].rearrange("p c t -> p (c t)"))
+
         w_codes, w_sc = {}, {}
 
-        def quantize_weight(key, scalar_cols=0):
+        def quantize_weight(key, scalar_cols):
             w_codes[key] = held([P, PASS], U32, "codes_%s_%d_%d" % key)
             w_sc[key] = held([P, PASS], U8, "scales_%s_%d_%d" % key)
             width = PASS // len(w_raw[key])
-            for part, raw in enumerate(w_raw[key]):
+            cut = width - scalar_cols
+            for piece, raw in enumerate(w_raw[key]):
                 grouped = work.tile([P, width, PACK], BF16, name="w_grouped", bufs=3, align_bytes=64)
-                cut = width - scalar_cols
-                if cut > 0:
-                    nc.vector.tensor_copy(
-                        grouped[:, :cut, :].rearrange("p (c n) i -> p c i n", n=4),
-                        raw[:, :, :cut].rearrange("p i (c n) -> p c i n", n=4),
-                    )
-                if cut < width:
-                    nc.scalar.copy(
-                        grouped[:, cut:, :].rearrange("p (c n) i -> p c i n", n=4),
-                        raw[:, :, cut:].rearrange("p i (c n) -> p c i n", n=4),
-                    )
-                cols = slice(part * width, (part + 1) * width)
-                nc.vector.quantize_mx(
-                    out=w_codes[key][:, cols].bitcast(FP8X4),
-                    scales=w_sc[key][:, cols],
-                    in_=grouped[:].rearrange("p c i -> p (c i)"),
-                )
+                nc.vector.tensor_copy(innermost(grouped[:, :cut, :], 4), outermost(raw[:, :, :cut], 4))
+                if scalar_cols:
+                    nc.scalar.copy(innermost(grouped[:, cut:, :], 4), outermost(raw[:, :, cut:], 4))
+                cols = slice(piece * width, (piece + 1) * width)
+                quantize(w_codes[key][:, cols], w_sc[key][:, cols], grouped)
 
         picked_w, picked_sc = {}, {}
 
         def gather(jq):
-            part = offsets[:, jq * SLICE // 16 : (jq + 1) * SLICE // 16]
+            part = offsets[:, jq * SLICE // LIST_ROWS : (jq + 1) * SLICE // LIST_ROWS]
             for a in range(2):
                 picked_w[(a, jq)] = held([P, SLICE], U32, "picked_w%d_%d" % (a, jq))
                 nc.vector.tensor_copy(picked_w[(a, jq)][:], tab_w[a][:].indirect(part))
@@ -219,116 +214,86 @@ def tile_list_spirometry_breath_curve_kernel(
                 w3_sc_raw[:, b * N : (b + 1) * N].rearrange("p (o q t) -> p o t q", t=PACK, q=16),
             )
 
-        def join(step, total, place):
-            b, jt = step
+        def join(step, total):
             both = psum.tile([P, PACK, P], F32, name="both", bufs=3)
             for t in range(PACK):
                 nc.tensor.matmul(both[:, t, :], wave_t[step][:, t, :], ident[:], start=True, stop=False, is_transpose=True)
                 nc.tensor.matmul(both[:, t, :], tanh_t[step][:, t, :], ident[:], start=False, stop=True, is_transpose=True)
-            nc.vector.scalar_tensor_tensor(
-                total[:, :, place * P : (place + 1) * P],
-                both[:],
-                -1.0,
-                alt_sb[(b, jt)],
-                ALU.add,
-                ALU.add,
-            )
+            nc.vector.scalar_tensor_tensor(total, both[:], -1.0, alt_sb[step], ALU.add, ALU.add)
 
         def quantize_h(b, total, cols):
             width = cols.stop - cols.start
             grouped = work.tile([P, width, PACK], BF16, name="h_grouped", bufs=3, align_bytes=64)
             nc.vector.tensor_tensor(
-                grouped[:].rearrange("p (c n) t -> p c t n", n=4),
-                total[:].rearrange("p t (c n) -> p c t n", n=4),
-                gains[:, b, :].unsqueeze(1).unsqueeze(3).to_broadcast([P, width // 4, PACK, 4]),
+                innermost(grouped[:], 2),
+                outermost(total[:], 2),
+                gains[:, b, :].unsqueeze(1).unsqueeze(3).to_broadcast([P, width // 2, PACK, 2]),
                 ALU.mult,
             )
-            nc.vector.quantize_mx(
-                out=h_codes[b][:, cols].bitcast(FP8X4), scales=h_sc[b][:, cols], in_=grouped[:].rearrange("p c t -> p (c t)")
-            )
+            quantize(h_codes[b][:, cols], h_sc[b][:, cols], grouped)
 
         out_rows = out_0.rearrange("(p t) j -> p t j", t=PACK)
         out_words = out_1[0].rearrange("p m t -> p (m t)").bitcast(I32)
 
-        def features(cols, late):
+        def features(cols):
             width = cols.stop - cols.start
-            part = P if late else width
-            per_bank = PASS // part
-            y = work.tile([P, PACK, width], F32, name="y", bufs=5)
-            grouped = work.tile([P, width, PACK], BF16, name="y_grouped", bufs=3, align_bytes=64)
-            for j0 in range(0, width, part):
-                moving = slice(cols.start + j0, cols.start + j0 + part)
-                for t0 in range(0, PACK, per_bank):
-                    acc = psum.tile([P, per_bank, part], F32, name="acc_y", tag="sine_then_y", bufs=3)
-                    for t in range(t0, t0 + per_bank):
-                        for b in range(2):
-                            nc.tensor.matmul_mx(
-                                out=acc[:, t - t0, :],
-                                lhsT=w3_w[b][:, t * 2 * P : (t + 1) * 2 * P].bitcast(FP4X4),
-                                lhsT_scale=w3_sc[b][:, t * P : (t + 1) * P],
-                                rhs=h_codes[b][:, moving].bitcast(FP8X4),
-                                rhs_scale=h_sc[b][:, moving],
-                                start=(b == 0),
-                                stop=(b == 1),
-                            )
-                    if late:
-                        nc.scalar.copy(grouped[:, j0 : j0 + P, :], acc[:].rearrange("p t j -> p j t"))
-                        nc.scalar.copy(y[:, :, j0 : j0 + P], acc[:])
-                    else:
-                        nc.scalar.copy(y[:, t0 : t0 + per_bank, :], acc[:])
-            if not late:
-                nc.vector.tensor_copy(
-                    grouped[:].rearrange("p (c n) t -> p c t n", n=4), y[:].rearrange("p t (c n) -> p c t n", n=4)
-                )
-            nc.vector.quantize_mx(
-                out=y_codes[:, cols].bitcast(FP8X4), scales=y_sc[:, cols], in_=grouped[:].rearrange("p c t -> p (c t)")
-            )
+            per_bank = PASS // width
+            y = work.tile([P, PACK, width], F32, name="y", bufs=4)
+            grouped = work.tile([P, width, PACK], BF16, name="y_grouped", bufs=2, align_bytes=64)
+            for t0 in range(0, PACK, per_bank):
+                acc = psum.tile([P, per_bank, width], F32, name="acc_y", tag="sine_then_y", bufs=3)
+                for t in range(t0, t0 + per_bank):
+                    for b in range(2):
+                        nc.tensor.matmul_mx(
+                            out=acc[:, t - t0, :],
+                            lhsT=w3_w[b][:, t * 2 * P : (t + 1) * 2 * P].bitcast(FP4X4),
+                            lhsT_scale=w3_sc[b][:, t * P : (t + 1) * P],
+                            rhs=h_codes[b][:, cols].bitcast(FP8X4),
+                            rhs_scale=h_sc[b][:, cols],
+                            start=(b == 0),
+                            stop=(b == 1),
+                        )
+                nc.scalar.copy(y[:, t0 : t0 + per_bank, :], acc[:])
+            nc.vector.tensor_copy(innermost(grouped[:], 4), outermost(y[:], 4))
+            quantize(y_codes[:, cols], y_sc[:, cols], grouped)
             nc.sync.dma_start(out_rows[:, :, cols], y[:])
-            if cols.stop in CODE_STORES:
-                done = slice(CODE_STORES[cols.stop], cols.stop)
+            if cols.stop % CODE_STORE == 0:
+                done = slice(cols.stop - CODE_STORE, cols.stop)
                 nc.sync.dma_start(out_words[:, done], y_codes[:, done].bitcast(I32))
 
-        TANH_AHEAD, SINE_AHEAD, SINE_FIRST, Y_LAG = 2, 4, 7, 5
-        steps = [(b, jt) for b, first, tiles in GROUPS for jt in range(first, first + tiles)]
-        sines = steps
-        quantize_weight(("w2", 0, 0), 96)
-        for step in sines[:SINE_FIRST]:
+        groups = [(0, jt, 2) for jt in range(0, 8, 2)] + [(1, jt, 2) for jt in range(0, 6, 2)] + [(1, 6, 1), (1, 7, 1)]
+        steps = [(b, jt) for b, first, tiles in groups for jt in range(first, first + tiles)]
+        quantize_weight(("w2", 0, 0), SCALAR_COLS)
+        for step in steps[:SINE_FIRST]:
             sine_branch(step)
         quantize_weight(("w1", 0, 0), 0)
         quantize_weight(("w1", 1, 0), 0)
         gather(0)
+        for b in range(2):
+            deal_w3(b)
         for step in steps[:TANH_AHEAD]:
             tanh_branch(step)
-        extras = {
-            0: lambda: (gather(1),),
-            1: lambda: (quantize_weight(("w2", 0, 1), 0),),
-            2: lambda: (gather(2),),
-            3: lambda: (quantize_weight(("w1", 0, 1), 0),),
-            4: lambda: (gather(3),),
-            5: lambda: (quantize_weight(("w1", 1, 1), 0),),
-            6: lambda: (deal_w3(0),),
-            7: lambda: (deal_w3(1),),
-        }
+
+        later_weights = [("w2", 0, 1), ("w1", 0, 1), ("w1", 1, 1)]
         count = 0
-        ready = []
-        for b, first, tiles in GROUPS:
+        for b, first, tiles in groups:
             total = work.tile([P, PACK, tiles * P], F32, name="total", bufs=3)
             for place in range(tiles):
-                if count in extras:
-                    extras[count]()
+                if count < 2 * len(later_weights):
+                    if count % 2 == 0:
+                        gather(count // 2 + 1)
+                    else:
+                        quantize_weight(later_weights[count // 2], 0)
                 if count + TANH_AHEAD < len(steps):
                     tanh_branch(steps[count + TANH_AHEAD])
-                join(steps[count], total, place)
+                join(steps[count], total[:, :, place * P : (place + 1) * P])
                 if SINE_FIRST <= count + SINE_AHEAD < len(steps):
-                    sine_branch(sines[count + SINE_AHEAD])
+                    sine_branch(steps[count + SINE_AHEAD])
                 count += 1
-            cols = slice(first * P, (first + tiles) * P)
-            quantize_h(b, total, cols)
+            quantize_h(b, total, slice(first * P, (first + tiles) * P))
+
+        for b, first, tiles in groups:
             if b == 1:
-                ready.append((cols, first >= SCALAR_FROM))
-                if len(ready) > Y_LAG:
-                    features(*ready.pop(0))
-        for cols, late in ready:
-            features(cols, late)
+                features(slice(first * P, (first + tiles) * P))
         for q in range(QUADS):
             nc.sync.dma_start(out_2[0, 4 * q : 4 * q + 4, :].bitcast(I32), y_sc[32 * q : 32 * q + 4, :].bitcast(I32))

import math
from contextlib import ExitStack

import concourse.mybir as mybir
from concourse.masks import make_identity

K, K2, H, N, T, S = 1024, 512, 1024, 512, 2048, 1024
FLOPS = 2 * S * (K * H + K2 * H + H * N)

F32 = mybir.dt.float32
BF16 = mybir.dt.bfloat16
I32 = mybir.dt.int32
U32 = mybir.dt.uint32
U16 = mybir.dt.uint16
U8 = mybir.dt.uint8
FP8X4 = mybir.dt.float8_e4m3fn_x4
FP4X4 = mybir.dt.float4_e2m1fn_x4
ACT = mybir.ActivationFunctionType
ALU = mybir.AluOpType

P = 128
PACK = 4
PASS = P * PACK
QUADS = 4
SLICE = 256
LIST_ROWS = 16
TANH_AHEAD = 2
SINE_AHEAD = 4
SINE_FIRST = 6
SCALAR_COLS = 96
CODE_STORE = 512


def tile_list_spirometry_breath_curve_kernel(
    tc, tab_words, tab_scales, offs, xs_words, xs_scales, w1, w2, alt, gain, w3_words, w3_scales, out_0, out_1, out_2
):
    nc = tc.nc
    with ExitStack() as ctx:
        keep = ctx.enter_context(tc.tile_pool(name="keep", bufs=1))
        work = ctx.enter_context(tc.tile_pool(name="work", bufs=2))
        psum = ctx.enter_context(tc.psum_pool(name="psum", bufs=2))

        def held(shape, dtype, name):
            return keep.tile(shape, dtype, name=name, align_bytes=64)

        offsets = keep.tile([P, S // LIST_ROWS], U16, name="offsets")
        nc.sync.dma_start(offsets[:], offs)

        xs_sc = held([P, S], U8, "xs_sc")
        tab_sc = held([P, T], U8, "tab_sc")
        w3_sc_raw = held([P, 2 * N], U8, "w3_sc_raw")
        for plane in (xs_sc, tab_sc, w3_sc_raw):
            nc.gpsimd.memset(plane[:].bitcast(I32), 0)

        ident = held([P, P], F32, "ident")
        make_identity(nc, ident[:])

        zero_in = held([P, 1], F32, "zero_in")
        zero = held([P, 1], F32, "zero")
        phase = held([P, 1], F32, "phase")
        root2 = held([P, 1], F32, "root2")
        nc.vector.memset(zero_in[:], 0.0)
        nc.scalar.activation(zero[:], zero_in[:], ACT.Silu)
        nc.vector.tensor_scalar(phase[:], zero[:], math.pi / 8, None, ALU.add)
        nc.vector.tensor_scalar(root2[:], zero[:], math.sqrt(2.0), None, ALU.add)

        xs_w = held([P, S], U32, "xs_w")
        tab_w = [held([P, T], U32, "tab_w%d" % a) for a in range(2)]
        w3_raw = held([P, 2 * 2 * N], U8, "w3_raw")
        gains = held([P, 2, PACK], F32, "gains")
        w_raw, alt_sb = {}, {}

        def load_weight(name, w, a, b, pieces):
            width = PASS // pieces
            w_raw[(name, a, b)] = []
            for piece in range(pieces):
                raw = work.tile([P, PACK, width], F32, name="w_raw%d" % pieces, bufs=5 if pieces == 1 else 2)
                rows = w[a * PASS : (a + 1) * PASS, b * PASS + piece * width : b * PASS + (piece + 1) * width]
                nc.sync.dma_start(raw[:], rows.rearrange("(p i) c -> p i c", i=PACK))
                w_raw[(name, a, b)].append(raw)

        def load_alt(b, first, tiles):
            rows = held([P, PACK, tiles * P], F32, "alt_%d_%d" % (b, first))
            src = alt[b * PASS : (b + 1) * PASS, first * P : (first + tiles) * P]
            nc.sync.dma_start(rows[:], src.rearrange("(p t) j -> p t j", t=PACK))
            for jt in range(tiles):
                alt_sb[(b, first + jt)] = rows[:, :, jt * P : (jt + 1) * P]

        def load_xs(cols):
            src = xs_words[0].rearrange("p c i -> p (c i)").bitcast(I32)
            nc.sync.dma_start(xs_w[:, cols].bitcast(I32), src[:, cols])

        def load_table(a):
            nc.sync.dma_start(tab_w[a][:].bitcast(I32), tab_words[a].rearrange("p c i -> p (c i)").bitcast(I32))

        load_weight("w2", w2, 0, 0, 2)
        load_xs(slice(0, SLICE))
        for q in range(QUADS):
            nc.sync.dma_start(xs_sc[32 * q : 32 * q + 4, :].bitcast(I32), xs_scales[0, 4 * q : 4 * q + 4, :].bitcast(I32))
        nc.sync.dma_start(
            w3_raw[:].bitcast(I32).rearrange("p (a n) -> p a n", a=2), w3_words.rearrange("a p n -> p a n").bitcast(I32)
        )
        load_xs(slice(SLICE, S))
        load_table(0)
        for q in range(QUADS):
            nc.sync.dma_start(tab_sc[32 * q : 32 * q + 8, :].bitcast(I32), tab_scales[:, 4 * q : 4 * q + 4, :].bitcast(I32))
        load_weight("w1", w1, 0, 0, 1)
        load_weight("w1", w1, 1, 0, 1)
        load_table(1)
        load_weight("w2", w2, 0, 1, 1)
        load_alt(0, 0, 2)
        nc.sync.dma_start(gains[:], gain.rearrange("(b p t) -> p b t", b=2, t=PACK))
        for q in range(QUADS):
            nc.sync.dma_start(
                w3_sc_raw[32 * q : 32 * q + 4, :].bitcast(I32).rearrange("r (a n) -> r a n", a=2),
                w3_scales[:, 4 * q : 4 * q + 4, :].rearrange("a r n -> r a n").bitcast(I32),
            )
        load_alt(0, 2, 2)
        load_weight("w1", w1, 0, 1, 1)
        load_alt(0, 4, 4)
        load_weight("w1", w1, 1, 1, 1)
        load_alt(1, 0, 4)
        load_alt(1, 4, 4)

        def innermost(rows, run):
            return rows.rearrange("p (c n) t -> p c t n", n=run)

        def outermost(rows, run):
            return rows.rearrange("p t (c n) -> p c t n", n=run)

        def quantize(codes, scales, grouped):
            nc.vector.quantize_mx(out=codes.bitcast(FP8X4), scales=scales, in_=grouped[:].rearrange("p c t -> p (c t)"))

        w_codes, w_sc = {}, {}

        def quantize_weight(key, scalar_cols):
            w_codes[key] = held([P, PASS], U32, "codes_%s_%d_%d" % key)
            w_sc[key] = held([P, PASS], U8, "scales_%s_%d_%d" % key)
            width = PASS // len(w_raw[key])
            cut = width - scalar_cols
            for piece, raw in enumerate(w_raw[key]):
                grouped = work.tile([P, width, PACK], BF16, name="w_grouped", bufs=3, align_bytes=64)
                nc.vector.tensor_copy(innermost(grouped[:, :cut, :], 4), outermost(raw[:, :, :cut], 4))
                if scalar_cols:
                    nc.scalar.copy(innermost(grouped[:, cut:, :], 4), outermost(raw[:, :, cut:], 4))
                cols = slice(piece * width, (piece + 1) * width)
                quantize(w_codes[key][:, cols], w_sc[key][:, cols], grouped)

        picked_w, picked_sc = {}, {}

        def gather(jq):
            part = offsets[:, jq * SLICE // LIST_ROWS : (jq + 1) * SLICE // LIST_ROWS]
            for a in range(2):
                picked_w[(a, jq)] = held([P, SLICE], U32, "picked_w%d_%d" % (a, jq))
                nc.vector.tensor_copy(picked_w[(a, jq)][:], tab_w[a][:].indirect(part))
            picked_sc[jq] = held([P, SLICE], U8, "picked_sc%d" % jq)
            nc.vector.tensor_copy(picked_sc[jq][:], tab_sc[:].indirect(part))

        tanh_t, wave_t = {}, {}

        def tanh_branch(step):
            b, jt = step
            jq, cols = jt // 2, slice((jt % 2) * P, (jt % 2 + 1) * P)
            acc = psum.tile([P, PASS], F32, name="acc_tanh", bufs=2)
            for a in (1, 0):
                nc.tensor.matmul_mx(
                    out=acc[:],
                    lhsT=picked_w[(a, jq)][:, cols].bitcast(FP8X4),
                    lhsT_scale=picked_sc[jq][4 * a : P, cols],
                    rhs=w_codes[("w1", a, b)][:].bitcast(FP8X4),
                    rhs_scale=w_sc[("w1", a, b)][:],
                    start=(a == 1),
                    stop=(a == 0),
                )
            tanh_t[step] = work.tile([P, PACK, P], F32, name="tanh_t", bufs=4)
            nc.scalar.activation(tanh_t[step][:], acc[:].rearrange("j (p t) -> j t p", t=PACK), ACT.Tanh)

        def sine_branch(step):
            b, jt = step
            cols = slice(jt * P, (jt + 1) * P)
            acc = psum.tile([P, PASS], F32, name="acc_sine", tag="sine_then_y", bufs=3)
            nc.tensor.matmul_mx(
                out=acc[:],
                lhsT=xs_w[:, cols].bitcast(FP8X4),
                lhsT_scale=xs_sc[:, cols],
                rhs=w_codes[("w2", 0, b)][:].bitcast(FP8X4),
                rhs_scale=w_sc[("w2", 0, b)][:],
                start=True,
                stop=True,
            )
            quarter = work.tile([P, PACK, P], F32, name="quarter", bufs=2)
            nc.scalar.activation(
                quarter[:], acc[:].rearrange("j (p t) -> j t p", t=PACK), ACT.Sin, bias=phase[:], scale=0.25
            )
            squared = work.tile([P, PACK, P], F32, name="squared", bufs=2)
            nc.scalar.activation(squared[:], quarter[:], ACT.Square)
            wave_t[step] = work.tile([P, PACK, P], F32, name="wave_t", bufs=9)
            nc.scalar.activation(wave_t[step][:], squared[:], ACT.Square, bias=root2[:], scale=-2.0 * math.sqrt(2.0))

        h_codes = [held([P, S], U32, "h_codes%d" % b) for b in range(2)]
        h_sc = [held([P, S], U8, "h_sc%d" % b) for b in range(2)]
        y_codes = held([P, S], U32, "y_codes")
        y_sc = held([P, S], U8, "y_sc")
        w3_w = [held([P, 2 * N], U8, "w3_w%d" % b) for b in range(2)]
        w3_sc = [held([P, N], U8, "w3_sc%d" % b) for b in range(2)]

        def deal_w3(b):
            nc.scalar.copy(
                w3_w[b][:].bitcast(U16).rearrange("p (t o q) -> p o t q", t=PACK, q=8),
                w3_raw[:, b * 2 * N : (b + 1) * 2 * N].bitcast(U16).rearrange("p (o q t) -> p o t q", t=PACK, q=8),
            )
            nc.vector.tensor_copy(
                w3_sc[b][:].rearrange("p (t o q) -> p o t q", t=PACK, q=16),
                w3_sc_raw[:, b * N : (b + 1) * N].rearrange("p (o q t) -> p o t q", t=PACK, q=16),
            )

        def join(step, total):
            both = psum.tile([P, PACK, P], F32, name="both", bufs=3)
            for t in range(PACK):
                nc.tensor.matmul(both[:, t, :], wave_t[step][:, t, :], ident[:], start=True, stop=False, is_transpose=True)
                nc.tensor.matmul(both[:, t, :], tanh_t[step][:, t, :], ident[:], start=False, stop=True, is_transpose=True)
            nc.vector.scalar_tensor_tensor(total, both[:], -1.0, alt_sb[step], ALU.add, ALU.add)

        def quantize_h(b, total, cols):
            width = cols.stop - cols.start
            grouped = work.tile([P, width, PACK], BF16, name="h_grouped", bufs=3, align_bytes=64)
            nc.vector.tensor_tensor(
                innermost(grouped[:], 2),
                outermost(total[:], 2),
                gains[:, b, :].unsqueeze(1).unsqueeze(3).to_broadcast([P, width // 2, PACK, 2]),
                ALU.mult,
            )
            quantize(h_codes[b][:, cols], h_sc[b][:, cols], grouped)

        out_rows = out_0.rearrange("(p t) j -> p t j", t=PACK)
        out_words = out_1[0].rearrange("p m t -> p (m t)").bitcast(I32)

        def features(cols):
            width = cols.stop - cols.start
            per_bank = PASS // width
            y = work.tile([P, PACK, width], F32, name="y", bufs=4)
            grouped = work.tile([P, width, PACK], BF16, name="y_grouped", bufs=2, align_bytes=64)
            for t0 in range(0, PACK, per_bank):
                acc = psum.tile([P, per_bank, width], F32, name="acc_y", tag="sine_then_y", bufs=3)
                for t in range(t0, t0 + per_bank):
                    for b in range(2):
                        nc.tensor.matmul_mx(
                            out=acc[:, t - t0, :],
                            lhsT=w3_w[b][:, t * 2 * P : (t + 1) * 2 * P].bitcast(FP4X4),
                            lhsT_scale=w3_sc[b][:, t * P : (t + 1) * P],
                            rhs=h_codes[b][:, cols].bitcast(FP8X4),
                            rhs_scale=h_sc[b][:, cols],
                            start=(b == 0),
                            stop=(b == 1),
                        )
                nc.scalar.copy(y[:, t0 : t0 + per_bank, :], acc[:])
            nc.vector.tensor_copy(innermost(grouped[:], 4), outermost(y[:], 4))
            quantize(y_codes[:, cols], y_sc[:, cols], grouped)
            nc.sync.dma_start(out_rows[:, :, cols], y[:])
            if cols.stop % CODE_STORE == 0:
                done = slice(cols.stop - CODE_STORE, cols.stop)
                nc.sync.dma_start(out_words[:, done], y_codes[:, done].bitcast(I32))

        groups = [(0, jt, 2) for jt in range(0, 8, 2)] + [(1, jt, 2) for jt in range(0, 6, 2)] + [(1, 6, 1), (1, 7, 1)]
        steps = [(b, jt) for b, first, tiles in groups for jt in range(first, first + tiles)]
        quantize_weight(("w2", 0, 0), SCALAR_COLS)
        for step in steps[:SINE_FIRST]:
            sine_branch(step)
        quantize_weight(("w1", 0, 0), 0)
        quantize_weight(("w1", 1, 0), 0)
        gather(0)
        for b in range(2):
            deal_w3(b)
        for step in steps[:TANH_AHEAD]:
            tanh_branch(step)

        later_weights = [("w2", 0, 1), ("w1", 0, 1), ("w1", 1, 1)]
        count = 0
        for b, first, tiles in groups:
            total = work.tile([P, PACK, tiles * P], F32, name="total", bufs=3)
            for place in range(tiles):
                if count < 2 * len(later_weights):
                    if count % 2 == 0:
                        gather(count // 2 + 1)
                    else:
                        quantize_weight(later_weights[count // 2], 0)
                if count + TANH_AHEAD < len(steps):
                    tanh_branch(steps[count + TANH_AHEAD])
                join(steps[count], total[:, :, place * P : (place + 1) * P])
                if SINE_FIRST <= count + SINE_AHEAD < len(steps):
                    sine_branch(steps[count + SINE_AHEAD])
                count += 1
            quantize_h(b, total, slice(first * P, (first + tiles) * P))

        for b, first, tiles in groups:
            if b == 1:
                features(slice(first * P, (first + tiles) * P))
        for q in range(QUADS):
            nc.sync.dma_start(out_2[0, 4 * q : 4 * q + 4, :].bitcast(I32), y_sc[32 * q : 32 * q + 4, :].bitcast(I32))
